import numpy as np
import ml_dtypes


def mxq(x, axis, fmt="e4m3"):
    dtype, down = {"e4m3": (ml_dtypes.float8_e4m3fn, 7), "e5m2": (ml_dtypes.float8_e5m2, 14)}[fmt]
    v = np.moveaxis(np.asarray(x, np.float32).astype(ml_dtypes.bfloat16).astype(np.float64), axis, -1)
    blocks = v.reshape(v.shape[:-1] + (-1, 32))
    amax = np.abs(blocks).max(-1, keepdims=True)
    byte = np.maximum(np.where(amax > 0, np.frexp(amax)[1] - 1 + 127, 0) - down, 1)
    scale = np.exp2(byte - 127.0)
    codes = (blocks / scale).astype(np.float32).astype(dtype).astype(np.float64)
    return np.moveaxis((codes * scale).reshape(v.shape), -1, axis)


WIDE = False


def mx_kscale(k):
    if not WIDE:
        return np.ones(k)
    levels = np.array([10, -10, 5, -5, 0])
    if k % 512:
        return np.exp2(np.random.permutation(np.resize(levels, k // 32))).repeat(32)
    a = np.empty((k // 512, 16))
    for p in range(k // 512):
        a[p, :8] = np.random.permutation(np.resize(levels, 8))
        for g in range(8):
            far = levels[np.abs(levels - a[p, g]) >= 10]
            a[p, g + 8] = far[np.random.randint(len(far))]
    return np.exp2(a.ravel()).repeat(32)


def f64(x):
    return np.asarray(x).astype(np.float64)


def striped(idx):
    return np.tile(idx.reshape(-1, 16).T, (8, 1)).astype(np.uint16)


def unstriped(offs):
    return offs[:16].T.reshape(-1).astype(np.int64)


E2M1 = np.array([0.0, 0.5, 1.0, 1.5, 2.0, 3.0, 4.0, 6.0, -0.0, -0.5, -1.0, -1.5, -2.0, -3.0, -4.0, -6.0])


def pack_weight(w, fmt):
    k, n = w.shape
    w = f64(np.asarray(w, np.float32).astype(ml_dtypes.bfloat16)).reshape(k // 32, 32, n)
    amax = np.abs(w).max(1)
    if fmt == "e4m3":
        byte = np.frexp(amax)[1] - 1 + 127 - 7
    else:
        mant, ex = np.frexp(amax / 6.0)
        byte = np.where(mant > 0.5, ex, ex - 1) + 127
    byte = np.clip(np.where(amax > 0, byte, 1), 1, 254)
    scaled = (w * np.exp2(127.0 - byte)[:, None, :]).reshape(k, n).astype(np.float32)
    by_word = np.ascontiguousarray(scaled.reshape(k // 512, 128, 4, n).transpose(0, 1, 3, 2))
    if fmt == "e4m3":
        words = by_word.astype(ml_dtypes.float8_e4m3fn).view(np.uint8)
    else:
        c = by_word.astype(ml_dtypes.float4_e2m1fn).view(np.uint8) & 0xF
        words = (c[..., 0::2] | (c[..., 1::2] << 4)).reshape(k // 512, 128, 2 * n)
    return np.ascontiguousarray(words), np.ascontiguousarray(byte.astype(np.uint8).reshape(k // 512, 16, n))


def unpack_weight(words, scales, fmt):
    g, _, n = scales.shape
    words = np.ascontiguousarray(words).reshape(g, 128, n, -1)
    if fmt == "e4m3":
        vals = words.view(ml_dtypes.float8_e4m3fn).astype(np.float64)
    else:
        nib = np.empty((g, 128, n, 4), np.uint8)
        nib[..., 0::2] = words & 0xF
        nib[..., 1::2] = words >> 4
        vals = E2M1[nib]
    vals = vals * np.repeat(np.exp2(scales.astype(np.float64) - 127.0), 8, axis=1)[..., None]
    return vals.transpose(0, 1, 3, 2).reshape(g * 512, n)


def gelu(v):
    return 0.5 * v * (1.0 + np.tanh(np.sqrt(2.0 / np.pi) * (v + 0.044715 * v**3)))


def striped8(idx):
    return np.concatenate([v.reshape(-1, 16).T for v in idx]).astype(np.uint16)


def unstriped8(offs):
    return np.stack([offs[16 * g:16 * g + 16].T.reshape(-1) for g in range(8)]).astype(np.int64)


def heads(h, wgt, idx8):
    r = np.arange(h.shape[0])
    return wgt[r // 4 % 128] * h[r[:, None], idx8[r % 512 // 64]]


K, H, N, T, S, P = 1536, 1024, 768, 4096, 1024, 512


def setup_inputs():
    n = np.random.standard_normal
    s = mx_kscale(K)[:, None]
    u = mx_kscale(H)[:, None]
    tab_words, tab_scales = pack_weight(n((K, T)) * s, "e4m3")
    w1_words, w1_scales = pack_weight(1.5 * n((K, H)) / np.sqrt(K) / s, "e2m1")
    return {
        "tab_words": tab_words, "tab_scales": tab_scales,
        "offs": striped(np.random.permutation(T)[:S]),
        "w1_words": w1_words, "w1_scales": w1_scales,
        "sc": np.random.uniform(0.3, 0.55, H).astype(np.float32),
        "offs2": striped8(np.stack([np.random.permutation(S)[:P] for _ in range(8)])),
        "wga": np.repeat(np.random.uniform(0.5, 2.0, (8, P)), 16, axis=0).astype(np.float32),
        "offs3": striped8(np.stack([np.random.permutation(S)[:P] for _ in range(8)])),
        "wgb": np.repeat(np.random.uniform(0.5, 2.0, (8, P)), 16, axis=0).astype(np.float32),
        "age": np.random.uniform(-0.7, 0.7, (H, P)).astype(np.float32),
        "gain": (np.exp(0.3 * n(H)) * u[:, 0]).astype(np.float32),
        "w2": (2.0 * n((H, N)) / np.sqrt(H) / u).astype(np.float32),
    }


def reference(tab_words, tab_scales, offs, w1_words, w1_scales, sc, offs2, wga, offs3, wgb, age, gain, w2):
    v = unpack_weight(tab_words, tab_scales, "e4m3")[:, unstriped(offs)]
    w1 = unpack_weight(w1_words, w1_scales, "e2m1")
    h = f64(sc)[:, None] * np.tanh(w1.T @ v)
    xa = heads(h, f64(wga), unstriped8(offs2))
    xb = heads(h, f64(wgb), unstriped8(offs3))
    both = xa + xb
    z = f64(gain)[:, None] * (both * np.cos(both + f64(age)))
    out = mxq(f64(w2), 0, "e4m3").T @ mxq(z, 0, "e4m3")
    return out

@@ -1,0 +1,289 @@
+import math
+from contextlib import ExitStack
+
+import concourse.mybir as mybir
+
+K, H, N, T, S, M = 1536, 1024, 768, 4096, 1024, 512
+FLOPS = 2 * K * H * S + 2 * H * N * M
+
+F32 = mybir.dt.float32
+BF16 = mybir.dt.bfloat16
+I32 = mybir.dt.int32
+U32 = mybir.dt.uint32
+U16 = mybir.dt.uint16
+U8 = mybir.dt.uint8
+FP8X4 = mybir.dt.float8_e4m3fn_x4
+FP4X4 = mybir.dt.float4_e2m1fn_x4
+ACT = mybir.ActivationFunctionType
+MULT = mybir.AluOpType.mult
+ADD = mybir.AluOpType.add
+
+P = 128
+PACK = 4
+K_PASSES = K // (P * PACK)
+H_PASSES = H // (P * PACK)
+SLICES = H // P
+BANK = 512
+HALVES = S // BANK
+BANKS = 8
+LIST_ROWS = 16
+N_TILES = N // P
+W2_PIECE = 384
+STEP = 512
+CHUNKS = [(0, 256), (256, 128), (384, 128)]
+
+
+def tile_list_tutor_pupil_copying_kernel(
+    tc, tab_words, tab_scales, offs, w1_words, w1_scales, sc, offs2, wga, offs3, wgb, age, gain, w2, out
+):
+    nc = tc.nc
+    with ExitStack() as ctx:
+        lists = ctx.enter_context(tc.tile_pool(name="lists", bufs=1))
+        keep = ctx.enter_context(tc.tile_pool(name="keep", bufs=1))
+        ring = ctx.enter_context(tc.tile_pool(name="ring", bufs=2))
+        psum = ctx.enter_context(tc.psum_pool(name="psum", bufs=1))
+
+        def kept(shape, dtype, tag):
+            return keep.tile(shape, dtype, name=tag, tag=tag, align_bytes=64)
+
+        table_list = lists.tile([P, S // LIST_ROWS], U16, name="table_list")
+        tutor_list = lists.tile([P, M // LIST_ROWS], U16, name="tutor_list")
+        pupil_list = lists.tile([P, M // LIST_ROWS], U16, name="pupil_list")
+        nc.sync.dma_start(table_list[:], offs)
+        nc.sync.dma_start(tutor_list[:], offs2)
+        nc.sync.dma_start(pupil_list[:], offs3)
+
+        scale_window = kept([P, T], U8, "scale_window")
+        nc.vector.memset(scale_window[:].bitcast(I32), 0)
+        nc.scalar.dma_start(
+            scale_window[0:96:2, :].bitcast(I32), tab_scales.rearrange("a q t -> q a t").bitcast(I32)
+        )
+
+        w1_scale_raw = kept([P, K_PASSES, H], U8, "w1_scale_raw")
+        nc.gpsimd.memset(w1_scale_raw[:].rearrange("p a c -> p (a c)").bitcast(U32), 0)
+        for quad in range(4):
+            nc.gpsimd.dma_start(
+                w1_scale_raw[32 * quad : 32 * quad + 4, :, :].bitcast(I32),
+                w1_scales[:, 4 * quad : 4 * quad + 4, :].rearrange("a r c -> r a c").bitcast(I32),
+            )
+        table_planes = kept([P, K_PASSES, S], U8, "table_planes")
+        nc.vector.memset(table_planes[:].rearrange("p a c -> p (a c)").bitcast(I32), 0)
+
+        table = [kept([P, T], I32, "table%d" % a) for a in range(K_PASSES)]
+        w1_raw = kept([P, K_PASSES, 2 * H], U8, "w1_raw")
+        for a in range(K_PASSES):
+            nc.sync.dma_start(table[a][:], tab_words[a].rearrange("p t i -> p (t i)").bitcast(I32))
+            if a == 0:
+                nc.sync.dma_start(w1_raw[:].bitcast(I32), w1_words.rearrange("a p c -> p a c").bitcast(I32))
+
+        picked_scales = kept([P, S], U8, "picked_scales")
+        nc.vector.tensor_copy(picked_scales[:], scale_window[:].indirect(table_list[:]))
+        for quad in range(4):
+            nc.scalar.dma_start(
+                table_planes[32 * quad : 32 * quad + 4, :, :].bitcast(I32),
+                picked_scales[24 * quad : 24 * quad + 24 : 2, :].bitcast(I32),
+            )
+        weights = kept([P, 2, M], F32, "scale_window")
+        nc.sync.dma_start(weights[:, 0, :], wga)
+        nc.sync.dma_start(weights[:, 1, :], wgb)
+
+        w1_planes = kept([P, K_PASSES, H], U8, "w1_planes")
+        nc.vector.tensor_copy(
+            w1_planes[:].rearrange("p a (b i q) -> p (a b) q i", i=PACK, q=P),
+            w1_scale_raw[:].rearrange("p a (b q i) -> p (a b) q i", i=PACK, q=P),
+        )
+        w1_codes = [kept([P, 2 * H], U8, "w1_codes%d" % a) for a in range(K_PASSES)]
+        for a in range(K_PASSES):
+            nc.vector.tensor_copy(
+                w1_codes[a][:].rearrange("p (b i q e) -> p b q i e", i=PACK, q=P, e=2),
+                w1_raw[:, a, :].rearrange("p (b q i e) -> p b q i e", i=PACK, q=P, e=2),
+            )
+        picked = {}
+        picked_tags = [["picked00", "picked01"], ["w1_scale_raw", "w1_raw"], ["picked20", "picked21"]]
+        for a in range(K_PASSES):
+            for half in range(HALVES):
+                picked[a, half] = kept([P, BANK], U32, picked_tags[a][half])
+                cols = slice(half * BANK // LIST_ROWS, (half + 1) * BANK // LIST_ROWS)
+                nc.vector.tensor_copy(picked[a, half][:], table[a][:].bitcast(U32).indirect(table_list[:, cols]))
+
+        early = kept([P, 2 * SLICES + PACK * M], F32, "table0")
+        sc_cols = early[:, 0:SLICES].rearrange("p (b i) -> p b i", i=PACK)
+        gain_cols = early[:, SLICES : 2 * SLICES].rearrange("p (b i) -> p b i", i=PACK)
+        nc.sync.dma_start(sc_cols, sc.rearrange("(b p i) -> p b i", p=P, i=PACK))
+        nc.sync.dma_start(gain_cols, gain.rearrange("(b p i) -> p b i", p=P, i=PACK))
+        ages = [
+            early[:, 2 * SLICES :].rearrange("p (i m) -> p i m", i=PACK),
+            kept([P, PACK, M], F32, "picked_scales")[:],
+        ]
+        w2_raw = [kept([P, PACK, N], F32, "table%d" % (b + 1)) for b in range(H_PASSES)]
+        for b in range(H_PASSES):
+            rows = slice(b * P * PACK, (b + 1) * P * PACK)
+            nc.sync.dma_start(ages[b], age[rows, :].rearrange("(p i) m -> p i m", i=PACK))
+            nc.sync.dma_start(w2_raw[b][:], w2[rows, :].rearrange("(p i) n -> p i n", i=PACK))
+        gain_sc = kept([P, H_PASSES, PACK], F32, "gain_sc")
+        nc.vector.tensor_tensor(gain_sc[:], gain_cols, sc_cols, MULT)
+
+        def bank_tile(index, width):
+            return psum.tile([P, width], F32, name="bank%d" % index, tag="bank%d" % index)
+
+        features = [kept([P, S], F32, "features%d" % s) for s in range(SLICES)]
+
+        def first_pass(acc, s, half, a):
+            nc.tensor.matmul_mx(
+                acc[:],
+                lhsT=w1_codes[a][:, 2 * P * s : 2 * P * (s + 1)].bitcast(FP4X4),
+                lhsT_scale=w1_planes[:, a, P * s : P * (s + 1)],
+                rhs=picked[a, half][:].bitcast(FP8X4),
+                rhs_scale=table_planes[:, a, half * BANK : (half + 1) * BANK],
+                start=(a == 0),
+                stop=(a == K_PASSES - 1),
+            )
+
+        def bound(acc, s, half):
+            nc.scalar.activation(features[s][:, half * BANK : (half + 1) * BANK], acc[:], ACT.Tanh)
+
+        wave = BANKS // HALVES
+        accs = {(s, half): bank_tile(HALVES * s + half, BANK) for s in range(wave) for half in range(HALVES)}
+        for a in range(K_PASSES):
+            for half in range(HALVES):
+                for s in range(wave):
+                    first_pass(accs[s, half], s, half, a)
+        for s in range(wave):
+            for half in range(HALVES):
+                bound(accs[s, half], s, half)
+        for s in range(wave, SLICES):
+            for half in range(HALVES):
+                acc = bank_tile(HALVES * (s - wave) + half, BANK)
+                for a in range(K_PASSES):
+                    first_pass(acc, s, half, a)
+                bound(acc, s, half)
+
+        steps = [
+            (0, [0, 1], 0, 256),
+            (0, [2, 3], 0, 256),
+            (1, [0, 1], 0, 256),
+            (1, [2, 3], 0, 256),
+            (0, [0, 1], 256, 256),
+            (0, [2, 3], 256, 256),
+            (1, [0, 1, 2, 3], 256, 128),
+            (1, [0, 1], 384, 128),
+            (1, [2, 3], 384, 128),
+        ]
+        w2_parts_after = {2: [0, 1], 3: [2, 3], 4: [4, 5, 6], 5: [7]}
+
+        taken, sums, cosines, rounded, woven = {}, {}, {}, {}, {}
+        w2_codes, w2_planes, w2_woven, out_banks = {}, {}, {}, {}
+
+        def pick(k):
+            b, members, m0, width = steps[k]
+            cols = slice(m0 // LIST_ROWS, (m0 + width) // LIST_ROWS)
+            for side in range(2):
+                taken[k, side] = ring.tile(
+                    [P, len(members), width], F32, name="taken%d" % side, tag="taken%d" % side, bufs=1
+                )
+            for j, i in enumerate(members):
+                for side, side_list in enumerate((tutor_list, pupil_list)):
+                    nc.vector.tensor_tensor(
+                        taken[k, side][:, j, :],
+                        features[PACK * b + i][:].indirect(side_list[:, cols]),
+                        weights[:, side, m0 : m0 + width],
+                        MULT,
+                    )
+
+        def cosine(k):
+            b, members, m0, width = steps[k]
+            sums[k] = ring.tile([P, len(members), width], F32, name="sums", tag="sums")
+            nc.vector.tensor_tensor(sums[k][:], taken[k, 0][:], taken[k, 1][:], ADD)
+            angle = ring.tile([P, len(members), width], F32, name="angle", tag="angle")
+            for j, i in enumerate(members):
+                nc.vector.scalar_tensor_tensor(
+                    angle[:, j, :], sums[k][:, j, :], sc_cols[:, b, i : i + 1], ages[b][:, i, m0 : m0 + width], MULT, ADD
+                )
+            cosines[k] = kept([P, len(members), width], F32, picked_tags[k % K_PASSES][1])
+            nc.scalar.activation(cosines[k][:], angle[:], ACT.Abs)
+            nc.scalar.activation(cosines[k][:], cosines[k][:], ACT.Sin, bias=math.pi / 2, scale=-1.0)
+
+        def weave_w2(part):
+            piece, c0 = part // 2, part % 2 * W2_PIECE // 2
+            b, n0 = piece // 2, piece % 2 * W2_PIECE + c0
+            if c0 == 0:
+                w2_woven[piece] = ring.tile([P, W2_PIECE, PACK], BF16, name="w2_woven", tag="w2_woven", align_bytes=64)
+            nc.scalar.copy(
+                w2_woven[piece][:, c0 : c0 + W2_PIECE // 2, :].rearrange("p (c e) i -> p c i e", e=4),
+                w2_raw[b][:, :, n0 : n0 + W2_PIECE // 2].rearrange("p i (c e) -> p c i e", e=4),
+            )
+            if c0 > 0:
+                w2_codes[piece] = kept([P, W2_PIECE], U32, "w2_codes%d" % piece)
+                w2_planes[piece] = kept([P, W2_PIECE], U8, "w2_planes%d" % piece)
+                nc.vector.quantize_mx(
+                    w2_codes[piece][:].bitcast(FP8X4),
+                    w2_planes[piece][:],
+                    w2_woven[piece][:].rearrange("p c i -> p (c i)"),
+                )
+
+        def product(k):
+            b, members, m0, width = steps[k]
+            if members[0] == 0:
+                rounded[b, m0] = ring.tile([P, PACK, width], BF16, name="rounded", tag="rounded")
+            for j, i in enumerate(members):
+                nc.vector.scalar_tensor_tensor(
+                    rounded[b, m0][:, i, :], cosines[k][:, j, :], gain_sc[:, b, i : i + 1], sums[k][:, j, :], MULT, MULT
+                )
+            if members[-1] == PACK - 1:
+                woven[k] = ring.tile([P, width, PACK], BF16, name="woven", tag="woven", align_bytes=64)
+                weave = nc.vector.tensor_copy if k == len(steps) - 1 else nc.scalar.copy
+                weave(
+                    woven[k][:].rearrange("p (c e) i -> p c i e", e=4),
+                    rounded[b, m0][:].rearrange("p i (c e) -> p c i e", e=4),
+                )
+
+        def second_passes(b, chunk, codes, planes, first_col):
+            m0, width = CHUNKS[chunk]
+            per_bank = 2 if width == 256 else 3
+            last_chunk = chunk == len(CHUNKS) - 1
+            for group in range(N_TILES // per_bank):
+                if b == 0:
+                    out_banks[chunk, group] = bank_tile(len(out_banks), per_bank * width)
+                acc = out_banks[chunk, group]
+                cols = slice(m0 - first_col, m0 - first_col + width)
+                for j in range(per_bank):
+                    piece, c0 = divmod((group * per_bank + j) * P, W2_PIECE)
+                    nc.tensor.matmul_mx(
+                        acc[:, j * width : (j + 1) * width],
+                        lhsT=w2_codes[2 * b + piece][:, c0 : c0 + P].bitcast(FP8X4),
+                        lhsT_scale=w2_planes[2 * b + piece][:, c0 : c0 + P],
+                        rhs=codes[:, cols].bitcast(FP8X4),
+                        rhs_scale=planes[:, cols],
+                        start=(b == 0 and j == 0),
+                        stop=(b == H_PASSES - 1 and j == per_bank - 1),
+                    )
+                if b == H_PASSES - 1:
+                    staged = kept([P, per_bank, width], F32, "staged%d%d" % (chunk, group))
+                    flat = staged[:].rearrange("p t m -> p (t m)")
+                    if last_chunk and group == 0:
+                        nc.vector.tensor_copy(flat, acc[:])
+                    else:
+                        nc.scalar.copy(flat, acc[:])
+                    rows = slice(group * per_bank * P, (group + 1) * per_bank * P)
+                    nc.sync.dma_start(out[rows, m0 : m0 + width].rearrange("(t p) m -> p t m", p=P), staged[:])
+
+        def multiply(k):
+            b, members, m0, width = steps[k]
+            codes = kept([P, width], U32, "x_codes%d" % k)
+            planes = kept([P, width], U8, "x_planes%d" % k)
+            nc.vector.quantize_mx(codes[:].bitcast(FP8X4), planes[:], woven[k][:].rearrange("p c i -> p (c i)"))
+            for chunk, (c0, cw) in enumerate(CHUNKS):
+                if m0 <= c0 < m0 + width:
+                    second_passes(b, chunk, codes, planes, m0)
+
+        for k in range(len(steps) + 2):
+            if k < len(steps):
+                pick(k)
+            if k >= 2:
+                product(k - 2)
+            if k < len(steps):
+                cosine(k)
+            for part in w2_parts_after.get(k, []):
+                weave_w2(part)
+            if k - 2 in woven:
+                multiply(k - 2)

@@ -2,6 +2,7 @@ import math
 from contextlib import ExitStack
 
 import concourse.mybir as mybir
+from concourse.masks import make_identity
 
 K, H, N, T, S, M = 1536, 1024, 768, 4096, 1024, 512
 FLOPS = 2 * K * H * S + 2 * H * N * M
@@ -26,6 +27,8 @@ SLICES = H // P
 BANK = 512
 HALVES = S // BANK
 BANKS = 8
+MX_BANKS = 6
+TURNED_STEPS = 7
 LIST_ROWS = 16
 N_TILES = N // P
 W2_PIECE = 384
@@ -53,21 +56,29 @@ def tile_list_tutor_pupil_copying_kernel(
         nc.sync.dma_start(tutor_list[:], offs2)
         nc.sync.dma_start(pupil_list[:], offs3)
 
+        sc_cols = kept([P, H_PASSES, PACK], F32, "sc_cols")
+        pupil_weights = kept([P, M], F32, "pupil_weights")
+        nc.sync.dma_start(sc_cols[:], sc.rearrange("(b p i) -> p b i", p=P, i=PACK))
+        nc.sync.dma_start(pupil_weights[:], wgb)
+
         scale_window = kept([P, T], U8, "scale_window")
+        w1_scale_rows = kept([P, H], U8, "w1_scale_rows")
+        planes1 = kept([P, K_PASSES, S + H], U8, "planes1")
         nc.vector.memset(scale_window[:].bitcast(I32), 0)
+        nc.gpsimd.memset(w1_scale_rows[:].bitcast(U32), 0)
+        nc.gpsimd.memset(planes1[:].rearrange("p a c -> p (a c)").bitcast(U32), 0)
         nc.scalar.dma_start(
             scale_window[0:96:2, :].bitcast(I32), tab_scales.rearrange("a q t -> q a t").bitcast(I32)
         )
+        nc.scalar.dma_start(
+            w1_scale_rows[0:96:2, :].bitcast(I32), w1_scales.rearrange("a q c -> q a c").bitcast(I32)
+        )
+        identity = kept([P, P], F32, "identity")
+        make_identity(nc, identity[:])
 
-        w1_scale_raw = kept([P, K_PASSES, H], U8, "w1_scale_raw")
-        nc.gpsimd.memset(w1_scale_raw[:].rearrange("p a c -> p (a c)").bitcast(U32), 0)
-        for quad in range(4):
-            nc.gpsimd.dma_start(
-                w1_scale_raw[32 * quad : 32 * quad + 4, :, :].bitcast(I32),
-                w1_scales[:, 4 * quad : 4 * quad + 4, :].rearrange("a r c -> r a c").bitcast(I32),
-            )
-        table_planes = kept([P, K_PASSES, S], U8, "table_planes")
-        nc.vector.memset(table_planes[:].rearrange("p a c -> p (a c)").bitcast(I32), 0)
+        warm = kept([P, 2], F32, "warm")
+        nc.vector.memset(warm[:, 0:1], 0.0)
+        nc.scalar.activation(warm[:, 1:2], warm[:, 0:1], ACT.Silu)
 
         table = [kept([P, T], I32, "table%d" % a) for a in range(K_PASSES)]
         w1_raw = kept([P, K_PASSES, 2 * H], U8, "w1_raw")
@@ -77,51 +88,52 @@ def tile_list_tutor_pupil_copying_kernel(
                 nc.sync.dma_start(w1_raw[:].bitcast(I32), w1_words.rearrange("a p c -> p a c").bitcast(I32))
 
         picked_scales = kept([P, S], U8, "picked_scales")
+        scale_rows = kept([P, S + H], U8, "scale_rows")
         nc.vector.tensor_copy(picked_scales[:], scale_window[:].indirect(table_list[:]))
+        nc.vector.tensor_copy(
+            scale_rows[:, S:].rearrange("p (b i q) -> p b i q", i=PACK, q=P),
+            w1_scale_rows[:].rearrange("p (b q i) -> p b i q", i=PACK, q=P),
+        )
+        nc.vector.tensor_copy(scale_rows[:, :S].bitcast(I32), picked_scales[:].bitcast(I32))
         for quad in range(4):
             nc.scalar.dma_start(
-                table_planes[32 * quad : 32 * quad + 4, :, :].bitcast(I32),
-                picked_scales[24 * quad : 24 * quad + 24 : 2, :].bitcast(I32),
+                planes1[32 * quad : 32 * quad + 4, :, :].bitcast(I32),
+                scale_rows[24 * quad : 24 * quad + 24 : 2, :].bitcast(I32),
             )
-        weights = kept([P, 2, M], F32, "scale_window")
-        nc.sync.dma_start(weights[:, 0, :], wga)
-        nc.sync.dma_start(weights[:, 1, :], wgb)
+        scaled_weights = [kept([P, M], F32, "scaled_weights%d" % s) for s in range(SLICES)]
+        for s in range(SLICES):
+            b, i = divmod(s, PACK)
+            nc.scalar.activation(scaled_weights[s][:], pupil_weights[:], ACT.Copy, scale=sc_cols[:, b, i : i + 1])
 
-        w1_planes = kept([P, K_PASSES, H], U8, "w1_planes")
-        nc.vector.tensor_copy(
-            w1_planes[:].rearrange("p a (b i q) -> p (a b) q i", i=PACK, q=P),
-            w1_scale_raw[:].rearrange("p a (b q i) -> p (a b) q i", i=PACK, q=P),
-        )
         w1_codes = [kept([P, 2 * H], U8, "w1_codes%d" % a) for a in range(K_PASSES)]
         for a in range(K_PASSES):
             nc.vector.tensor_copy(
-                w1_codes[a][:].rearrange("p (b i q e) -> p b q i e", i=PACK, q=P, e=2),
-                w1_raw[:, a, :].rearrange("p (b q i e) -> p b q i e", i=PACK, q=P, e=2),
+                w1_codes[a][:].rearrange("p (b i q e) -> p b i q e", i=PACK, q=P, e=2),
+                w1_raw[:, a, :].rearrange("p (b q i e) -> p b i q e", i=PACK, q=P, e=2),
             )
         picked = {}
-        picked_tags = [["picked00", "picked01"], ["w1_scale_raw", "w1_raw"], ["picked20", "picked21"]]
+        picked_tags = [["picked00", "picked01"], ["w1_raw", "picked11"], ["picked20", "picked21"]]
         for a in range(K_PASSES):
             for half in range(HALVES):
                 picked[a, half] = kept([P, BANK], U32, picked_tags[a][half])
                 cols = slice(half * BANK // LIST_ROWS, (half + 1) * BANK // LIST_ROWS)
                 nc.vector.tensor_copy(picked[a, half][:], table[a][:].bitcast(U32).indirect(table_list[:, cols]))
 
-        early = kept([P, 2 * SLICES + PACK * M], F32, "table0")
-        sc_cols = early[:, 0:SLICES].rearrange("p (b i) -> p b i", i=PACK)
-        gain_cols = early[:, SLICES : 2 * SLICES].rearrange("p (b i) -> p b i", i=PACK)
-        nc.sync.dma_start(sc_cols, sc.rearrange("(b p i) -> p b i", p=P, i=PACK))
-        nc.sync.dma_start(gain_cols, gain.rearrange("(b p i) -> p b i", p=P, i=PACK))
+        tutor_weights = kept([P, M], F32, "scale_rows")
+        nc.sync.dma_start(tutor_weights[:], wga)
+        early = kept([P, SLICES + PACK * M], F32, "table0")
+        gain_cols = early[:, 0:SLICES].rearrange("p (b i) -> p b i", i=PACK)
         ages = [
-            early[:, 2 * SLICES :].rearrange("p (i m) -> p i m", i=PACK),
-            kept([P, PACK, M], F32, "picked_scales")[:],
+            early[:, SLICES:].rearrange("p (i m) -> p i m", i=PACK),
+            kept([P, PACK, M], F32, "pupil_weights")[:],
         ]
         w2_raw = [kept([P, PACK, N], F32, "table%d" % (b + 1)) for b in range(H_PASSES)]
         for b in range(H_PASSES):
             rows = slice(b * P * PACK, (b + 1) * P * PACK)
             nc.sync.dma_start(ages[b], age[rows, :].rearrange("(p i) m -> p i m", i=PACK))
+            if b == 0:
+                nc.sync.dma_start(gain_cols, gain.rearrange("(b p i) -> p b i", p=P, i=PACK))
             nc.sync.dma_start(w2_raw[b][:], w2[rows, :].rearrange("(p i) n -> p i n", i=PACK))
-        gain_sc = kept([P, H_PASSES, PACK], F32, "gain_sc")
-        nc.vector.tensor_tensor(gain_sc[:], gain_cols, sc_cols, MULT)
 
         def bank_tile(index, width):
             return psum.tile([P, width], F32, name="bank%d" % index, tag="bank%d" % index)
@@ -132,9 +144,9 @@ def tile_list_tutor_pupil_copying_kernel(
             nc.tensor.matmul_mx(
                 acc[:],
                 lhsT=w1_codes[a][:, 2 * P * s : 2 * P * (s + 1)].bitcast(FP4X4),
-                lhsT_scale=w1_planes[:, a, P * s : P * (s + 1)],
+                lhsT_scale=planes1[:, a, S + P * s : S + P * (s + 1)],
                 rhs=picked[a, half][:].bitcast(FP8X4),
-                rhs_scale=table_planes[:, a, half * BANK : (half + 1) * BANK],
+                rhs_scale=planes1[:, a, half * BANK : (half + 1) * BANK],
                 start=(a == 0),
                 stop=(a == K_PASSES - 1),
             )
@@ -153,7 +165,7 @@ def tile_list_tutor_pupil_copying_kernel(
                 bound(accs[s, half], s, half)
         for s in range(wave, SLICES):
             for half in range(HALVES):
-                acc = bank_tile(HALVES * (s - wave) + half, BANK)
+                acc = bank_tile((HALVES * (s - wave) + half) % MX_BANKS, BANK)
                 for a in range(K_PASSES):
                     first_pass(acc, s, half, a)
                 bound(acc, s, half)
@@ -186,22 +198,47 @@ def tile_list_tutor_pupil_copying_kernel(
                     nc.vector.tensor_tensor(
                         taken[k, side][:, j, :],
                         features[PACK * b + i][:].indirect(side_list[:, cols]),
-                        weights[:, side, m0 : m0 + width],
+                        (tutor_weights, scaled_weights[PACK * b + i])[side][:, m0 : m0 + width],
                         MULT,
                     )
 
         def cosine(k):
             b, members, m0, width = steps[k]
             sums[k] = ring.tile([P, len(members), width], F32, name="sums", tag="sums")
-            nc.vector.tensor_tensor(sums[k][:], taken[k, 0][:], taken[k, 1][:], ADD)
-            angle = ring.tile([P, len(members), width], F32, name="angle", tag="angle")
             for j, i in enumerate(members):
                 nc.vector.scalar_tensor_tensor(
-                    angle[:, j, :], sums[k][:, j, :], sc_cols[:, b, i : i + 1], ages[b][:, i, m0 : m0 + width], MULT, ADD
+                    sums[k][:, j, :], taken[k, 0][:, j, :], sc_cols[:, b, i : i + 1], taken[k, 1][:, j, :], MULT, ADD
                 )
-            cosines[k] = kept([P, len(members), width], F32, picked_tags[k % K_PASSES][1])
-            nc.scalar.activation(cosines[k][:], angle[:], ACT.Abs)
-            nc.scalar.activation(cosines[k][:], cosines[k][:], ACT.Sin, bias=math.pi / 2, scale=-1.0)
+            cosines[k] = ring.tile([P, len(members), width], F32, name="cosines", tag="cosines")
+            size = ring.tile([P, len(members) * width], F32, name="size", tag="size")
+            if k < TURNED_STEPS:
+                blocks = [(j, i, c) for j, i in enumerate(members) for c in range(0, width, P)]
+                turned = bank_tile(7, BANK)
+                for n, (j, i, c) in enumerate(blocks):
+                    nc.tensor.matmul(
+                        turned[:, n * P : (n + 1) * P], ages[b][:, i, m0 + c : m0 + c + P], identity[:],
+                        start=(n == 0), stop=False, is_transpose=True,
+                    )
+                for n, (j, i, c) in enumerate(blocks):
+                    nc.tensor.matmul(
+                        turned[:, n * P : (n + 1) * P], sums[k][:, j, c : c + P], identity[:],
+                        start=False, stop=(n == len(blocks) - 1), is_transpose=True,
+                    )
+                nc.scalar.activation(size[:], turned[:], ACT.Abs)
+                back = bank_tile(6, BANK)
+                for n in range(len(blocks)):
+                    nc.tensor.transpose(back[:, n * P : (n + 1) * P], size[:, n * P : (n + 1) * P], identity[:])
+                source = back
+            else:
+                angle = ring.tile([P, len(members), width], F32, name="angle", tag="angle")
+                nc.vector.tensor_tensor(
+                    angle[:], sums[k][:], ages[b][:, members[0] : members[-1] + 1, m0 : m0 + width], ADD
+                )
+                nc.scalar.activation(size[:], angle[:].rearrange("p j m -> p (j m)"), ACT.Abs)
+                source = size
+            nc.scalar.activation(
+                cosines[k][:].rearrange("p j m -> p (j m)"), source[:], ACT.Sin, bias=math.pi / 2, scale=-1.0
+            )
 
         def weave_w2(part):
             piece, c0 = part // 2, part % 2 * W2_PIECE // 2
@@ -227,7 +264,7 @@ def tile_list_tutor_pupil_copying_kernel(
                 rounded[b, m0] = ring.tile([P, PACK, width], BF16, name="rounded", tag="rounded")
             for j, i in enumerate(members):
                 nc.vector.scalar_tensor_tensor(
-                    rounded[b, m0][:, i, :], cosines[k][:, j, :], gain_sc[:, b, i : i + 1], sums[k][:, j, :], MULT, MULT
+                    rounded[b, m0][:, i, :], cosines[k][:, j, :], gain_cols[:, b, i : i + 1], sums[k][:, j, :], MULT, MULT
                 )
             if members[-1] == PACK - 1:
                 woven[k] = ring.tile([P, width, PACK], BF16, name="woven", tag="woven", align_bytes=64)
@@ -243,7 +280,7 @@ def tile_list_tutor_pupil_copying_kernel(
             last_chunk = chunk == len(CHUNKS) - 1
             for group in range(N_TILES // per_bank):
                 if b == 0:
-                    out_banks[chunk, group] = bank_tile(len(out_banks), per_bank * width)
+                    out_banks[chunk, group] = bank_tile(len(out_banks) % MX_BANKS, per_bank * width)
                 acc = out_banks[chunk, group]
                 cols = slice(m0 - first_col, m0 - first_col + width)
                 for j in range(per_bank):

@@ -112,7 +112,7 @@ def tile_list_tutor_pupil_copying_kernel(
                 w1_raw[:, a, :].rearrange("p (b q i e) -> p b i q e", i=PACK, q=P, e=2),
             )
         picked = {}
-        picked_tags = [["picked00", "picked01"], ["w1_raw", "picked11"], ["picked20", "picked21"]]
+        picked_tags = [["scale_window", "w1_scale_rows"], ["w1_raw", "picked11"], ["picked20", "picked21"]]
         for a in range(K_PASSES):
             for half in range(HALVES):
                 picked[a, half] = kept([P, BANK], U32, picked_tags[a][half])
@@ -154,21 +154,20 @@ def tile_list_tutor_pupil_copying_kernel(
         def bound(acc, s, half):
             nc.scalar.activation(features[s][:, half * BANK : (half + 1) * BANK], acc[:], ACT.Tanh)
 
-        wave = BANKS // HALVES
-        accs = {(s, half): bank_tile(HALVES * s + half, BANK) for s in range(wave) for half in range(HALVES)}
-        for a in range(K_PASSES):
-            for half in range(HALVES):
-                for s in range(wave):
-                    first_pass(accs[s, half], s, half, a)
-        for s in range(wave):
-            for half in range(HALVES):
-                bound(accs[s, half], s, half)
-        for s in range(wave, SLICES):
-            for half in range(HALVES):
-                acc = bank_tile((HALVES * (s - wave) + half) % MX_BANKS, BANK)
-                for a in range(K_PASSES):
-                    first_pass(acc, s, half, a)
-                bound(acc, s, half)
+        for pair in range(SLICES // 2):
+            members = (2 * pair, 2 * pair + 1)
+            accs = {}
+            for s in members:
+                for half in range(HALVES):
+                    index = HALVES * s + half
+                    accs[s, half] = bank_tile(index if index < BANKS else (index - BANKS) % MX_BANKS, BANK)
+            for a in range(K_PASSES):
+                for half in range(HALVES):
+                    for s in members:
+                        first_pass(accs[s, half], s, half, a)
+            for s in members:
+                for half in range(HALVES):
+                    bound(accs[s, half], s, half)
 
         steps = [
             (0, [0, 1], 0, 256),
@@ -246,8 +245,8 @@ def tile_list_tutor_pupil_copying_kernel(
             if c0 == 0:
                 w2_woven[piece] = ring.tile([P, W2_PIECE, PACK], BF16, name="w2_woven", tag="w2_woven", align_bytes=64)
             nc.scalar.copy(
-                w2_woven[piece][:, c0 : c0 + W2_PIECE // 2, :].rearrange("p (c e) i -> p c i e", e=4),
-                w2_raw[b][:, :, n0 : n0 + W2_PIECE // 2].rearrange("p i (c e) -> p c i e", e=4),
+                w2_woven[piece][:, c0 : c0 + W2_PIECE // 2, :],
+                w2_raw[b][:, :, n0 : n0 + W2_PIECE // 2].rearrange("p i c -> p c i"),
             )
             if c0 > 0:
                 w2_codes[piece] = kept([P, W2_PIECE], U32, "w2_codes%d" % piece)
@@ -269,10 +268,7 @@ def tile_list_tutor_pupil_copying_kernel(
             if members[-1] == PACK - 1:
                 woven[k] = ring.tile([P, width, PACK], BF16, name="woven", tag="woven", align_bytes=64)
                 weave = nc.vector.tensor_copy if k == len(steps) - 1 else nc.scalar.copy
-                weave(
-                    woven[k][:].rearrange("p (c e) i -> p c i e", e=4),
-                    rounded[b, m0][:].rearrange("p i (c e) -> p c i e", e=4),
-                )
+                weave(woven[k][:], rounded[b, m0][:].rearrange("p i c -> p c i"))
 
         def second_passes(b, chunk, codes, planes, first_col):
             m0, width = CHUNKS[chunk]

@@ -55,6 +55,8 @@ def tile_list_tutor_pupil_copying_kernel(
         nc.sync.dma_start(table_list[:], offs)
         nc.sync.dma_start(tutor_list[:], offs2)
         nc.sync.dma_start(pupil_list[:], offs3)
+        table = [kept([P, T], I32, "table%d" % a) for a in range(K_PASSES)]
+        nc.sync.dma_start(table[0][:], tab_words[0].rearrange("p t i -> p (t i)").bitcast(I32))
 
         sc_cols = kept([P, H_PASSES, PACK], F32, "sc_cols")
         pupil_weights = kept([P, M], F32, "pupil_weights")
@@ -64,9 +66,9 @@ def tile_list_tutor_pupil_copying_kernel(
         scale_window = kept([P, T], U8, "scale_window")
         w1_scale_rows = kept([P, H], U8, "w1_scale_rows")
         planes1 = kept([P, K_PASSES, S + H], U8, "planes1")
-        nc.vector.memset(scale_window[:].bitcast(I32), 0)
-        nc.gpsimd.memset(w1_scale_rows[:].bitcast(U32), 0)
-        nc.gpsimd.memset(planes1[:].rearrange("p a c -> p (a c)").bitcast(U32), 0)
+        nc.gpsimd.memset(scale_window[:].bitcast(U32), 0)
+        nc.vector.memset(w1_scale_rows[:].bitcast(I32), 0)
+        nc.vector.memset(planes1[:].rearrange("p a c -> p (a c)").bitcast(I32), 0)
         nc.scalar.dma_start(
             scale_window[0:96:2, :].bitcast(I32), tab_scales.rearrange("a q t -> q a t").bitcast(I32)
         )
@@ -80,12 +82,10 @@ def tile_list_tutor_pupil_copying_kernel(
         nc.vector.memset(warm[:, 0:1], 0.0)
         nc.scalar.activation(warm[:, 1:2], warm[:, 0:1], ACT.Silu)
 
-        table = [kept([P, T], I32, "table%d" % a) for a in range(K_PASSES)]
         w1_raw = kept([P, K_PASSES, 2 * H], U8, "w1_raw")
-        for a in range(K_PASSES):
+        nc.sync.dma_start(w1_raw[:].bitcast(I32), w1_words.rearrange("a p c -> p a c").bitcast(I32))
+        for a in range(1, K_PASSES):
             nc.sync.dma_start(table[a][:], tab_words[a].rearrange("p t i -> p (t i)").bitcast(I32))
-            if a == 0:
-                nc.sync.dma_start(w1_raw[:].bitcast(I32), w1_words.rearrange("a p c -> p a c").bitcast(I32))
 
         picked_scales = kept([P, S], U8, "picked_scales")
         scale_rows = kept([P, S + H], U8, "scale_rows")
@@ -95,7 +95,7 @@ def tile_list_tutor_pupil_copying_kernel(
             w1_scale_rows[:].rearrange("p (b q i) -> p b i q", i=PACK, q=P),
         )
         nc.vector.tensor_copy(scale_rows[:, :S].bitcast(I32), picked_scales[:].bitcast(I32))
-        for quad in range(4):
+        for quad in (0, 2, 1, 3):
             nc.scalar.dma_start(
                 planes1[32 * quad : 32 * quad + 4, :, :].bitcast(I32),
                 scale_rows[24 * quad : 24 * quad + 24 : 2, :].bitcast(I32),
@@ -121,19 +121,20 @@ def tile_list_tutor_pupil_copying_kernel(
 
         tutor_weights = kept([P, M], F32, "scale_rows")
         nc.sync.dma_start(tutor_weights[:], wga)
-        early = kept([P, SLICES + PACK * M], F32, "table0")
-        gain_cols = early[:, 0:SLICES].rearrange("p (b i) -> p b i", i=PACK)
-        ages = [
-            early[:, SLICES:].rearrange("p (i m) -> p i m", i=PACK),
-            kept([P, PACK, M], F32, "pupil_weights")[:],
-        ]
-        w2_raw = [kept([P, PACK, N], F32, "table%d" % (b + 1)) for b in range(H_PASSES)]
+        ages_and_gain = kept([P, SLICES + H_PASSES * PACK * M], F32, "table1")
+        gain_cols = ages_and_gain[:, 0:SLICES].rearrange("p (b i) -> p b i", i=PACK)
+        age_rows = ages_and_gain[:, SLICES:].rearrange("p (b i m) -> p b i m", b=H_PASSES, i=PACK)
+        ages = [age_rows[:, b, :, :] for b in range(H_PASSES)]
+        w2_rows = kept([P, H_PASSES, PACK, N], F32, "table2")
+        w2_raw = [w2_rows[:, b, :, :] for b in range(H_PASSES)]
         for b in range(H_PASSES):
             rows = slice(b * P * PACK, (b + 1) * P * PACK)
             nc.sync.dma_start(ages[b], age[rows, :].rearrange("(p i) m -> p i m", i=PACK))
             if b == 0:
                 nc.sync.dma_start(gain_cols, gain.rearrange("(b p i) -> p b i", p=P, i=PACK))
-            nc.sync.dma_start(w2_raw[b][:], w2[rows, :].rearrange("(p i) n -> p i n", i=PACK))
+        for b in range(H_PASSES):
+            rows = slice(b * P * PACK, (b + 1) * P * PACK)
+            nc.sync.dma_start(w2_raw[b], w2[rows, :].rearrange("(p i) n -> p i n", i=PACK))
 
         def bank_tile(index, width):
             return psum.tile([P, width], F32, name="bank%d" % index, tag="bank%d" % index)
@@ -154,13 +155,12 @@ def tile_list_tutor_pupil_copying_kernel(
         def bound(acc, s, half):
             nc.scalar.activation(features[s][:, half * BANK : (half + 1) * BANK], acc[:], ACT.Tanh)
 
-        for pair in range(SLICES // 2):
+        def first_stage(pair):
             members = (2 * pair, 2 * pair + 1)
             accs = {}
             for s in members:
                 for half in range(HALVES):
-                    index = HALVES * s + half
-                    accs[s, half] = bank_tile(index if index < BANKS else (index - BANKS) % MX_BANKS, BANK)
+                    accs[s, half] = bank_tile(HALVES * (s % 2) + half, BANK)
             for a in range(K_PASSES):
                 for half in range(HALVES):
                     for s in members:
@@ -169,18 +169,21 @@ def tile_list_tutor_pupil_copying_kernel(
                 for half in range(HALVES):
                     bound(accs[s, half], s, half)
 
+        first_stage(0)
+        first_stage(1)
+
         steps = [
             (0, [0, 1], 0, 256),
             (0, [2, 3], 0, 256),
+            (0, [0, 1], 256, 256),
             (1, [0, 1], 0, 256),
             (1, [2, 3], 0, 256),
-            (0, [0, 1], 256, 256),
             (0, [2, 3], 256, 256),
             (1, [0, 1, 2, 3], 256, 128),
-            (1, [0, 1], 384, 128),
-            (1, [2, 3], 384, 128),
+            (1, [0, 1, 2], 384, 128),
+            (1, [3], 384, 128),
         ]
-        w2_parts_after = {2: [0, 1], 3: [2, 3], 4: [4, 5, 6], 5: [7]}
+        w2_parts_after = {2: [0, 1], 3: [2, 3], 4: [4, 5], 5: [6, 7]}
 
         taken, sums, cosines, rounded, woven = {}, {}, {}, {}, {}
         w2_codes, w2_planes, w2_woven, out_banks = {}, {}, {}, {}
@@ -245,8 +248,8 @@ def tile_list_tutor_pupil_copying_kernel(
             if c0 == 0:
                 w2_woven[piece] = ring.tile([P, W2_PIECE, PACK], BF16, name="w2_woven", tag="w2_woven", align_bytes=64)
             nc.scalar.copy(
-                w2_woven[piece][:, c0 : c0 + W2_PIECE // 2, :],
-                w2_raw[b][:, :, n0 : n0 + W2_PIECE // 2].rearrange("p i c -> p c i"),
+                w2_woven[piece][:, c0 : c0 + W2_PIECE // 2, :].rearrange("p (c e) i -> p c i e", e=4),
+                w2_raw[b][:, :, n0 : n0 + W2_PIECE // 2].rearrange("p i (c e) -> p c i e", e=4),
             )
             if c0 > 0:
                 w2_codes[piece] = kept([P, W2_PIECE], U32, "w2_codes%d" % piece)
@@ -260,7 +263,7 @@ def tile_list_tutor_pupil_copying_kernel(
         def product(k):
             b, members, m0, width = steps[k]
             if members[0] == 0:
-                rounded[b, m0] = ring.tile([P, PACK, width], BF16, name="rounded", tag="rounded")
+                rounded[b, m0] = ring.tile([P, PACK, width], BF16, name="rounded", tag="rounded", bufs=3)
             for j, i in enumerate(members):
                 nc.vector.scalar_tensor_tensor(
                     rounded[b, m0][:, i, :], cosines[k][:, j, :], gain_cols[:, b, i : i + 1], sums[k][:, j, :], MULT, MULT
@@ -268,7 +271,10 @@ def tile_list_tutor_pupil_copying_kernel(
             if members[-1] == PACK - 1:
                 woven[k] = ring.tile([P, width, PACK], BF16, name="woven", tag="woven", align_bytes=64)
                 weave = nc.vector.tensor_copy if k == len(steps) - 1 else nc.scalar.copy
-                weave(woven[k][:], rounded[b, m0][:].rearrange("p i c -> p c i"))
+                weave(
+                    woven[k][:].rearrange("p (c e) i -> p c i e", e=4),
+                    rounded[b, m0][:].rearrange("p i (c e) -> p c i e", e=4),
+                )
 
         def second_passes(b, chunk, codes, planes, first_col):
             m0, width = CHUNKS[chunk]
@@ -316,6 +322,8 @@ def tile_list_tutor_pupil_copying_kernel(
                 product(k - 2)
             if k < len(steps):
                 cosine(k)
+            if k < 2:
+                first_stage(k + 2)
             for part in w2_parts_after.get(k, []):
                 weave_w2(part)
             if k - 2 in woven:

@@ -28,6 +28,7 @@ BANK = 512
 HALVES = S // BANK
 BANKS = 8
 MX_BANKS = 6
+FIRST_BANKS = 3
 TURNED_STEPS = 7
 LIST_ROWS = 16
 N_TILES = N // P
@@ -155,27 +156,20 @@ def tile_list_tutor_pupil_copying_kernel(
         def bound(acc, s, half):
             nc.scalar.activation(features[s][:, half * BANK : (half + 1) * BANK], acc[:], ACT.Tanh)
 
-        def first_stage(pair):
-            members = (2 * pair, 2 * pair + 1)
-            accs = {}
-            for s in members:
-                for half in range(HALVES):
-                    accs[s, half] = bank_tile(HALVES * (s % 2) + half, BANK)
-            for a in range(K_PASSES):
-                for half in range(HALVES):
-                    for s in members:
-                        first_pass(accs[s, half], s, half, a)
-            for s in members:
-                for half in range(HALVES):
-                    bound(accs[s, half], s, half)
+        def first_stage(s):
+            for half in range(HALVES):
+                acc = bank_tile((HALVES * s + half) % FIRST_BANKS, BANK)
+                for a in range(K_PASSES):
+                    first_pass(acc, s, half, a)
+                bound(acc, s, half)
 
         first_stage(0)
         first_stage(1)
 
         steps = [
-            (0, [0, 1], 0, 256),
+            (0, [0], 0, 512),
+            (0, [1], 0, 512),
             (0, [2, 3], 0, 256),
-            (0, [0, 1], 256, 256),
             (1, [0, 1], 0, 256),
             (1, [2, 3], 0, 256),
             (0, [2, 3], 256, 256),
@@ -185,7 +179,7 @@ def tile_list_tutor_pupil_copying_kernel(
         ]
         w2_parts_after = {2: [0, 1], 3: [2, 3], 4: [4, 5], 5: [6, 7]}
 
-        taken, sums, cosines, rounded, woven = {}, {}, {}, {}, {}
+        taken, sums, cosines, woven = {}, {}, {}, {}
         w2_codes, w2_planes, w2_woven, out_banks = {}, {}, {}, {}
 
         def pick(k):
@@ -260,20 +254,25 @@ def tile_list_tutor_pupil_copying_kernel(
                     w2_woven[piece][:].rearrange("p c i -> p (c i)"),
                 )
 
+        rounded = [kept([P, PACK, M], BF16, "rounded%d" % b) for b in range(H_PASSES)]
+
         def product(k):
             b, members, m0, width = steps[k]
-            if members[0] == 0:
-                rounded[b, m0] = ring.tile([P, PACK, width], BF16, name="rounded", tag="rounded", bufs=3)
             for j, i in enumerate(members):
                 nc.vector.scalar_tensor_tensor(
-                    rounded[b, m0][:, i, :], cosines[k][:, j, :], gain_cols[:, b, i : i + 1], sums[k][:, j, :], MULT, MULT
+                    rounded[b][:, i, m0 : m0 + width],
+                    cosines[k][:, j, :],
+                    gain_cols[:, b, i : i + 1],
+                    sums[k][:, j, :],
+                    MULT,
+                    MULT,
                 )
             if members[-1] == PACK - 1:
                 woven[k] = ring.tile([P, width, PACK], BF16, name="woven", tag="woven", align_bytes=64)
                 weave = nc.vector.tensor_copy if k == len(steps) - 1 else nc.scalar.copy
                 weave(
                     woven[k][:].rearrange("p (c e) i -> p c i e", e=4),
-                    rounded[b, m0][:].rearrange("p i (c e) -> p c i e", e=4),
+                    rounded[b][:, :, m0 : m0 + width].rearrange("p i (c e) -> p c i e", e=4),
                 )
 
         def second_passes(b, chunk, codes, planes, first_col):
@@ -322,8 +321,9 @@ def tile_list_tutor_pupil_copying_kernel(
                 product(k - 2)
             if k < len(steps):
                 cosine(k)
-            if k < 2:
-                first_stage(k + 2)
+            if k < 3:
+                first_stage(2 * k + 2)
+                first_stage(2 * k + 3)
             for part in w2_parts_after.get(k, []):
                 weave_w2(part)
             if k - 2 in woven:

import math
from contextlib import ExitStack

import concourse.mybir as mybir
from concourse.masks import make_identity

K, H, N, T, S, M = 1536, 1024, 768, 4096, 1024, 512
FLOPS = 2 * K * H * S + 2 * H * N * M

F32 = mybir.dt.float32
BF16 = mybir.dt.bfloat16
I32 = mybir.dt.int32
U32 = mybir.dt.uint32
U16 = mybir.dt.uint16
U8 = mybir.dt.uint8
FP8X4 = mybir.dt.float8_e4m3fn_x4
FP4X4 = mybir.dt.float4_e2m1fn_x4
ACT = mybir.ActivationFunctionType
MULT = mybir.AluOpType.mult
ADD = mybir.AluOpType.add

P = 128
PACK = 4
K_PASSES = K // (P * PACK)
H_PASSES = H // (P * PACK)
SLICES = H // P
BANK = 512
HALVES = S // BANK
BANKS = 8
MX_BANKS = 6
FIRST_BANKS = 3
TURNED_STEPS = 7
LIST_ROWS = 16
N_TILES = N // P
W2_PIECE = 384
STEP = 512
CHUNKS = [(0, 256), (256, 128), (384, 128)]


def tile_list_tutor_pupil_copying_kernel(
    tc, tab_words, tab_scales, offs, w1_words, w1_scales, sc, offs2, wga, offs3, wgb, age, gain, w2, out
):
    nc = tc.nc
    with ExitStack() as ctx:
        lists = ctx.enter_context(tc.tile_pool(name="lists", bufs=1))
        keep = ctx.enter_context(tc.tile_pool(name="keep", bufs=1))
        ring = ctx.enter_context(tc.tile_pool(name="ring", bufs=2))
        psum = ctx.enter_context(tc.psum_pool(name="psum", bufs=1))

        def kept(shape, dtype, tag):
            return keep.tile(shape, dtype, name=tag, tag=tag, align_bytes=64)

        table_list = lists.tile([P, S // LIST_ROWS], U16, name="table_list")
        tutor_list = lists.tile([P, M // LIST_ROWS], U16, name="tutor_list")
        pupil_list = lists.tile([P, M // LIST_ROWS], U16, name="pupil_list")
        nc.sync.dma_start(table_list[:], offs)
        nc.sync.dma_start(tutor_list[:], offs2)
        nc.sync.dma_start(pupil_list[:], offs3)
        table = [kept([P, T], I32, "table%d" % a) for a in range(K_PASSES)]
        nc.sync.dma_start(table[0][:], tab_words[0].rearrange("p t i -> p (t i)").bitcast(I32))

        sc_cols = kept([P, H_PASSES, PACK], F32, "sc_cols")
        pupil_weights = kept([P, M], F32, "pupil_weights")
        nc.sync.dma_start(sc_cols[:], sc.rearrange("(b p i) -> p b i", p=P, i=PACK))
        nc.sync.dma_start(pupil_weights[:], wgb)

        scale_window = kept([P, T], U8, "scale_window")
        w1_scale_rows = kept([P, H], U8, "w1_scale_rows")
        planes1 = kept([P, K_PASSES, S + H], U8, "planes1")
        nc.gpsimd.memset(scale_window[:].bitcast(U32), 0)
        nc.vector.memset(w1_scale_rows[:].bitcast(I32), 0)
        nc.vector.memset(planes1[:].rearrange("p a c -> p (a c)").bitcast(I32), 0)
        nc.scalar.dma_start(
            scale_window[0:96:2, :].bitcast(I32), tab_scales.rearrange("a q t -> q a t").bitcast(I32)
        )
        nc.scalar.dma_start(
            w1_scale_rows[0:96:2, :].bitcast(I32), w1_scales.rearrange("a q c -> q a c").bitcast(I32)
        )
        identity = kept([P, P], F32, "identity")
        make_identity(nc, identity[:])

        warm = kept([P, 2], F32, "warm")
        nc.vector.memset(warm[:, 0:1], 0.0)
        nc.scalar.activation(warm[:, 1:2], warm[:, 0:1], ACT.Silu)

        w1_raw = kept([P, K_PASSES, 2 * H], U8, "w1_raw")
        nc.sync.dma_start(w1_raw[:].bitcast(I32), w1_words.rearrange("a p c -> p a c").bitcast(I32))
        for a in range(1, K_PASSES):
            nc.sync.dma_start(table[a][:], tab_words[a].rearrange("p t i -> p (t i)").bitcast(I32))

        picked_scales = kept([P, S], U8, "picked_scales")
        scale_rows = kept([P, S + H], U8, "scale_rows")
        nc.vector.tensor_copy(picked_scales[:], scale_window[:].indirect(table_list[:]))
        nc.vector.tensor_copy(
            scale_rows[:, S:].rearrange("p (b i q) -> p b i q", i=PACK, q=P),
            w1_scale_rows[:].rearrange("p (b q i) -> p b i q", i=PACK, q=P),
        )
        nc.vector.tensor_copy(scale_rows[:, :S].bitcast(I32), picked_scales[:].bitcast(I32))
        for quad in (0, 2, 1, 3):
            nc.scalar.dma_start(
                planes1[32 * quad : 32 * quad + 4, :, :].bitcast(I32),
                scale_rows[24 * quad : 24 * quad + 24 : 2, :].bitcast(I32),
            )
        scaled_weights = [kept([P, M], F32, "scaled_weights%d" % s) for s in range(SLICES)]
        for s in range(SLICES):
            b, i = divmod(s, PACK)
            nc.scalar.activation(scaled_weights[s][:], pupil_weights[:], ACT.Copy, scale=sc_cols[:, b, i : i + 1])

        w1_codes = [kept([P, 2 * H], U8, "w1_codes%d" % a) for a in range(K_PASSES)]
        for a in range(K_PASSES):
            nc.vector.tensor_copy(
                w1_codes[a][:].rearrange("p (b i q e) -> p b i q e", i=PACK, q=P, e=2),
                w1_raw[:, a, :].rearrange("p (b q i e) -> p b i q e", i=PACK, q=P, e=2),
            )
        picked = {}
        picked_tags = [["scale_window", "w1_scale_rows"], ["w1_raw", "picked11"], ["picked20", "picked21"]]
        for a in range(K_PASSES):
            for half in range(HALVES):
                picked[a, half] = kept([P, BANK], U32, picked_tags[a][half])
                cols = slice(half * BANK // LIST_ROWS, (half + 1) * BANK // LIST_ROWS)
                nc.vector.tensor_copy(picked[a, half][:], table[a][:].bitcast(U32).indirect(table_list[:, cols]))

        tutor_weights = kept([P, M], F32, "scale_rows")
        nc.sync.dma_start(tutor_weights[:], wga)
        ages_and_gain = kept([P, SLICES + H_PASSES * PACK * M], F32, "table1")
        gain_cols = ages_and_gain[:, 0:SLICES].rearrange("p (b i) -> p b i", i=PACK)
        age_rows = ages_and_gain[:, SLICES:].rearrange("p (b i m) -> p b i m", b=H_PASSES, i=PACK)
        ages = [age_rows[:, b, :, :] for b in range(H_PASSES)]
        w2_rows = kept([P, H_PASSES, PACK, N], F32, "table2")
        w2_raw = [w2_rows[:, b, :, :] for b in range(H_PASSES)]
        for b in range(H_PASSES):
            rows = slice(b * P * PACK, (b + 1) * P * PACK)
            nc.sync.dma_start(ages[b], age[rows, :].rearrange("(p i) m -> p i m", i=PACK))
            if b == 0:
                nc.sync.dma_start(gain_cols, gain.rearrange("(b p i) -> p b i", p=P, i=PACK))
        for b in range(H_PASSES):
            rows = slice(b * P * PACK, (b + 1) * P * PACK)
            nc.sync.dma_start(w2_raw[b], w2[rows, :].rearrange("(p i) n -> p i n", i=PACK))

        def bank_tile(index, width):
            return psum.tile([P, width], F32, name="bank%d" % index, tag="bank%d" % index)

        features = [kept([P, S], F32, "features%d" % s) for s in range(SLICES)]

        def first_pass(acc, s, half, a):
            nc.tensor.matmul_mx(
                acc[:],
                lhsT=w1_codes[a][:, 2 * P * s : 2 * P * (s + 1)].bitcast(FP4X4),
                lhsT_scale=planes1[:, a, S + P * s : S + P * (s + 1)],
                rhs=picked[a, half][:].bitcast(FP8X4),
                rhs_scale=planes1[:, a, half * BANK : (half + 1) * BANK],
                start=(a == 0),
                stop=(a == K_PASSES - 1),
            )

        def bound(acc, s, half):
            nc.scalar.activation(features[s][:, half * BANK : (half + 1) * BANK], acc[:], ACT.Tanh)

        def first_stage(s):
            for half in range(HALVES):
                acc = bank_tile((HALVES * s + half) % FIRST_BANKS, BANK)
                for a in range(K_PASSES):
                    first_pass(acc, s, half, a)
                bound(acc, s, half)

        first_stage(0)
        first_stage(1)

        steps = [
            (0, [0], 0, 512),
            (0, [1], 0, 512),
            (0, [2, 3], 0, 256),
            (1, [0, 1], 0, 256),
            (1, [2, 3], 0, 256),
            (0, [2, 3], 256, 256),
            (1, [0, 1, 2, 3], 256, 128),
            (1, [0, 1, 2], 384, 128),
            (1, [3], 384, 128),
        ]
        w2_parts_after = {2: [0, 1], 3: [2, 3], 4: [4, 5], 5: [6, 7]}

        taken, sums, cosines, woven = {}, {}, {}, {}
        w2_codes, w2_planes, w2_woven, out_banks = {}, {}, {}, {}

        def pick(k):
            b, members, m0, width = steps[k]
            cols = slice(m0 // LIST_ROWS, (m0 + width) // LIST_ROWS)
            for side in range(2):
                taken[k, side] = ring.tile(
                    [P, len(members), width], F32, name="taken%d" % side, tag="taken%d" % side, bufs=1
                )
            for j, i in enumerate(members):
                for side, side_list in enumerate((tutor_list, pupil_list)):
                    nc.vector.tensor_tensor(
                        taken[k, side][:, j, :],
                        features[PACK * b + i][:].indirect(side_list[:, cols]),
                        (tutor_weights, scaled_weights[PACK * b + i])[side][:, m0 : m0 + width],
                        MULT,
                    )

        def cosine(k):
            b, members, m0, width = steps[k]
            sums[k] = ring.tile([P, len(members), width], F32, name="sums", tag="sums")
            for j, i in enumerate(members):
                nc.vector.scalar_tensor_tensor(
                    sums[k][:, j, :], taken[k, 0][:, j, :], sc_cols[:, b, i : i + 1], taken[k, 1][:, j, :], MULT, ADD
                )
            cosines[k] = ring.tile([P, len(members), width], F32, name="cosines", tag="cosines")
            size = ring.tile([P, len(members) * width], F32, name="size", tag="size")
            if k < TURNED_STEPS:
                blocks = [(j, i, c) for j, i in enumerate(members) for c in range(0, width, P)]
                turned = bank_tile(7, BANK)
                for n, (j, i, c) in enumerate(blocks):
                    nc.tensor.matmul(
                        turned[:, n * P : (n + 1) * P], ages[b][:, i, m0 + c : m0 + c + P], identity[:],
                        start=(n == 0), stop=False, is_transpose=True,
                    )
                for n, (j, i, c) in enumerate(blocks):
                    nc.tensor.matmul(
                        turned[:, n * P : (n + 1) * P], sums[k][:, j, c : c + P], identity[:],
                        start=False, stop=(n == len(blocks) - 1), is_transpose=True,
                    )
                nc.scalar.activation(size[:], turned[:], ACT.Abs)
                back = bank_tile(6, BANK)
                for n in range(len(blocks)):
                    nc.tensor.transpose(back[:, n * P : (n + 1) * P], size[:, n * P : (n + 1) * P], identity[:])
                source = back
            else:
                angle = ring.tile([P, len(members), width], F32, name="angle", tag="angle")
                nc.vector.tensor_tensor(
                    angle[:], sums[k][:], ages[b][:, members[0] : members[-1] + 1, m0 : m0 + width], ADD
                )
                nc.scalar.activation(size[:], angle[:].rearrange("p j m -> p (j m)"), ACT.Abs)
                source = size
            nc.scalar.activation(
                cosines[k][:].rearrange("p j m -> p (j m)"), source[:], ACT.Sin, bias=math.pi / 2, scale=-1.0
            )

        def weave_w2(part):
            piece, c0 = part // 2, part % 2 * W2_PIECE // 2
            b, n0 = piece // 2, piece % 2 * W2_PIECE + c0
            if c0 == 0:
                w2_woven[piece] = ring.tile([P, W2_PIECE, PACK], BF16, name="w2_woven", tag="w2_woven", align_bytes=64)
            nc.scalar.copy(
                w2_woven[piece][:, c0 : c0 + W2_PIECE // 2, :].rearrange("p (c e) i -> p c i e", e=4),
                w2_raw[b][:, :, n0 : n0 + W2_PIECE // 2].rearrange("p i (c e) -> p c i e", e=4),
            )
            if c0 > 0:
                w2_codes[piece] = kept([P, W2_PIECE], U32, "w2_codes%d" % piece)
                w2_planes[piece] = kept([P, W2_PIECE], U8, "w2_planes%d" % piece)
                nc.vector.quantize_mx(
                    w2_codes[piece][:].bitcast(FP8X4),
                    w2_planes[piece][:],
                    w2_woven[piece][:].rearrange("p c i -> p (c i)"),
                )

        rounded = [kept([P, PACK, M], BF16, "rounded%d" % b) for b in range(H_PASSES)]

        def product(k):
            b, members, m0, width = steps[k]
            for j, i in enumerate(members):
                nc.vector.scalar_tensor_tensor(
                    rounded[b][:, i, m0 : m0 + width],
                    cosines[k][:, j, :],
                    gain_cols[:, b, i : i + 1],
                    sums[k][:, j, :],
                    MULT,
                    MULT,
                )
            if members[-1] == PACK - 1:
                woven[k] = ring.tile([P, width, PACK], BF16, name="woven", tag="woven", align_bytes=64)
                weave = nc.vector.tensor_copy if k == len(steps) - 1 else nc.scalar.copy
                weave(
                    woven[k][:].rearrange("p (c e) i -> p c i e", e=4),
                    rounded[b][:, :, m0 : m0 + width].rearrange("p i (c e) -> p c i e", e=4),
                )

        def second_passes(b, chunk, codes, planes, first_col):
            m0, width = CHUNKS[chunk]
            per_bank = 2 if width == 256 else 3
            last_chunk = chunk == len(CHUNKS) - 1
            for group in range(N_TILES // per_bank):
                if b == 0:
                    out_banks[chunk, group] = bank_tile(len(out_banks) % MX_BANKS, per_bank * width)
                acc = out_banks[chunk, group]
                cols = slice(m0 - first_col, m0 - first_col + width)
                for j in range(per_bank):
                    piece, c0 = divmod((group * per_bank + j) * P, W2_PIECE)
                    nc.tensor.matmul_mx(
                        acc[:, j * width : (j + 1) * width],
                        lhsT=w2_codes[2 * b + piece][:, c0 : c0 + P].bitcast(FP8X4),
                        lhsT_scale=w2_planes[2 * b + piece][:, c0 : c0 + P],
                        rhs=codes[:, cols].bitcast(FP8X4),
                        rhs_scale=planes[:, cols],
                        start=(b == 0 and j == 0),
                        stop=(b == H_PASSES - 1 and j == per_bank - 1),
                    )
                if b == H_PASSES - 1:
                    staged = kept([P, per_bank, width], F32, "staged%d%d" % (chunk, group))
                    flat = staged[:].rearrange("p t m -> p (t m)")
                    if last_chunk and group == 0:
                        nc.vector.tensor_copy(flat, acc[:])
                    else:
                        nc.scalar.copy(flat, acc[:])
                    rows = slice(group * per_bank * P, (group + 1) * per_bank * P)
                    nc.sync.dma_start(out[rows, m0 : m0 + width].rearrange("(t p) m -> p t m", p=P), staged[:])

        def multiply(k):
            b, members, m0, width = steps[k]
            codes = kept([P, width], U32, "x_codes%d" % k)
            planes = kept([P, width], U8, "x_planes%d" % k)
            nc.vector.quantize_mx(codes[:].bitcast(FP8X4), planes[:], woven[k][:].rearrange("p c i -> p (c i)"))
            for chunk, (c0, cw) in enumerate(CHUNKS):
                if m0 <= c0 < m0 + width:
                    second_passes(b, chunk, codes, planes, m0)

        for k in range(len(steps) + 2):
            if k < len(steps):
                pick(k)
            if k >= 2:
                product(k - 2)
            if k < len(steps):
                cosine(k)
            if k < 3:
                first_stage(2 * k + 2)
                first_stage(2 * k + 3)
            for part in w2_parts_after.get(k, []):
                weave_w2(part)
            if k - 2 in woven:
                multiply(k - 2)
